import numpy as np, ml_dtypes
CORES = [8,136,40,168]
N = 4
import mx_ref
NC, G = 128, 4
C = np.float32(0.037)
BF = ml_dtypes.bfloat16
def cut(t, i, w=512):
    return t[:, w * i:w * i + w]
def tile(rs):
    return np.stack(rs, axis=2).reshape(128, -1).astype(BF)
def layer(w, X):
    out = []
    for i in range(G):
        for t in range(len(X)):
            p = mx_ref.matmul(mx_ref.quantize(cut(w, len(X) * i + t)), X[t])
            z = p if t == 0 else z + p
        out.append(z)
    return out
def masked(A, E):
    return [(e * (a > 0)) * C for a, e in zip(A, E)]
def setup_inputs(rng):
    def f(*shape):
        return mx_ref.flush((rng.standard_normal(shape, dtype=np.float32) * np.exp2(rng.integers(-2, 3, shape[:-1] + (1,)))).astype(BF))
    return {"x": f(N, 128, 512), "e": f(N, 128, 512), "a": f(N, 128, G * 512), "w": f(N, 128, 512), "v": f(N, 128, 4 * NC)}
def setup_inputs_blocks(rng):
    d = setup_inputs(rng)
    for k in ("x", "e", "a", "w", "v"): d[k] = mx_ref.spread(d[k], rng, 4)
    return d
def setup_inputs_wide(rng):
    d = setup_inputs(rng)
    for k in ("x", "e", "a", "w", "v"): d[k] = mx_ref.flush((d[k].astype(np.float32) * np.exp2(rng.integers(-6, 7, (N, 1, 1))).astype(np.float32)).astype(BF))
    return d
def setup_inputs_zeros(rng):
    d = setup_inputs(rng); v = d["x"].reshape(N, 128, -1, 4).copy()
    v[np.broadcast_to((rng.random((N, 1, v.shape[2], 1)) < 0.33), v.shape)] = 0
    d["x"] = v.reshape(d["x"].shape)
    return d
def reference(x, e, a, w, v):
    T = [mx_ref.quantize(tile(masked(layer(a[j], [mx_ref.quantize(x[j])]), layer(a[j], [mx_ref.quantize(e[j])])))) for j in range(N)]
    y = np.zeros((N, 128, N * 128), np.float32); z = np.zeros((N, 128, N * NC), np.float32)
    for r in range(N):
        qw = mx_ref.quantize(w[r]); qv = mx_ref.quantize(v[r])
        for j in range(N):
            y[r][:, 128 * j:128 * j + 128] = mx_ref.matmul(qw, T[j])
            p = mx_ref.matmul(T[j], qv)
            z[r][:, NC * j:NC * j + NC] = p
    return {"y": y, "z": z}

@@ -1,0 +1,148 @@
+from concourse.bass import DstId, RemoteDMATransfer
+from concourse.mybir import dt, AluOpType, ActivationFunctionType
+
+N = 4
+B = 128
+F = 4 * B
+BANK = 512
+C = 0.037
+CODES = "float8_e4m3fn_x4"
+
+SCRATCH = {
+    "xb": ("sbuf", [128, F], "bfloat16"),
+    "eb": ("sbuf", [128, F], "bfloat16"),
+    "ab": ("sbuf", [128, 4 * F], "bfloat16"),
+    "wb": ("sbuf", [128, F], "bfloat16"),
+    "vb": ("sbuf", [128, F], "bfloat16"),
+    "tb": ("sbuf", [128, F], "bfloat16"),
+    "mk": ("sbuf", [128, 4 * B], "float32"),
+    "oy": ("sbuf", [128, N * B], "float32"),
+    "oz": ("sbuf", [128, N * B], "float32"),
+    "xq": ("sbuf", [128, B], CODES), "xs": ("sbuf", [128, B], "uint8"),
+    "eq": ("sbuf", [128, B], CODES), "es": ("sbuf", [128, B], "uint8"),
+    "aq": ("sbuf", [128, 4 * B], CODES), "as_": ("sbuf", [128, 4 * B], "uint8"),
+    "wq": ("sbuf", [128, B], CODES), "ws": ("sbuf", [128, B], "uint8"),
+    "vq": ("sbuf", [128, B], CODES), "vs": ("sbuf", [128, B], "uint8"),
+    "tq": ("sbuf", [128, N * B], CODES), "ts": ("sbuf", [128, N * B], "uint8"),
+    "ps": ("psum", [128, 8 * BANK], "float32"),
+}
+SEMAPHORES = (
+    ["lx", "le", "la0", "la1", "lw", "lv"]
+    + ["qa%d" % i for i in range(4)] + ["qt", "qw", "qv"]
+    + ["u%d" % i for i in range(4)] + ["d%d" % i for i in range(4)]
+    + ["mk0", "mk1", "rt"]
+    + ["sent"] + ["arr%d" % j for j in range(N)]
+    + ["y%d" % j for j in range(N)] + ["z%d" % j for j in range(N)]
+    + ["cy%d" % k for k in range(3)] + ["cz%d" % k for k in range(3)]
+    + ["sty", "stz"]
+)
+
+
+def rank_program(g, core, T, topo):
+    me = T.rank_of(core)
+    if me is None:
+        return
+    S = T.sem
+
+    def blk(t, j, w=B):
+        return t[:, w * j:w * j + w]
+
+    def bank(b):
+        return T.ps[:, BANK * b:BANK * b + B]
+
+    order = [(me - k) % N for k in range(1, N)]
+    runs = [r for r in (list(range(0, me)), list(range(me + 1, N))) if r]
+    runs.sort(key=lambda r: max(order.index(j) for j in r))
+    run_of = {j: k for k, r in enumerate(runs) for j in r}
+
+    g.sync.dma_start(T.xb[:], T.x[:]).then_inc(S.lx, 16)
+    g.scalar.dma_start(T.eb[:], T.e[:]).then_inc(S.le, 16)
+    for h in range(2):
+        g.sync.dma_start(T.ab[:, 2 * F * h:2 * F * (h + 1)], T.a[:, 2 * F * h:2 * F * (h + 1)]).then_inc(S["la%d" % h], 16)
+    g.scalar.wait_ge(S.lx, 16)
+    g.scalar.dma_start(T.wb[:], T.w[:]).then_inc(S.lw, 16)
+    g.scalar.dma_start(T.vb[:], T.v[:]).then_inc(S.lv, 16)
+
+    v = g.vector
+    v.wait_ge(S.lx, 16)
+    v.quantize_mx(T.xq[:], T.xs[:], T.xb[:]).then_inc(S.qa0, 1)
+    v.wait_ge(S.le, 16)
+    v.quantize_mx(T.eq[:], T.es[:], T.eb[:]).then_inc(S.qa0, 1)
+    for h in range(2):
+        pair = (2 * h, 2 * h + 1)
+        v.wait_ge(S["la%d" % h], 16)
+        for i in pair:
+            v.quantize_mx(blk(T.aq, i), blk(T.as_, i), blk(T.ab, i, F)).then_inc(S["qa%d" % i], 1)
+        for i in pair:
+            v.wait_ge(S["u%d" % i], 1)
+            v.tensor_scalar(blk(T.mk, i), bank(i), 0.0, C, AluOpType.is_gt, AluOpType.mult).then_inc(S["mk%d" % h], 1)
+        v.wait_ge(S["mk%d" % h], 2)
+        for i in pair:
+            v.wait_ge(S["d%d" % i], 1)
+            v.tensor_tensor(T.tb[:, i:F:4], bank(4 + i), blk(T.mk, i), AluOpType.mult).then_inc(S.rt, 1)
+    v.wait_ge(S.rt, 4)
+    v.quantize_mx(blk(T.tq, me), blk(T.ts, me), T.tb[:]).then_inc(S.qt, 1)
+    v.wait_ge(S.lw, 16)
+    v.quantize_mx(T.wq[:], T.ws[:], T.wb[:]).then_inc(S.qw, 1)
+    v.wait_ge(S.lv, 16)
+    v.quantize_mx(T.vq[:], T.vs[:], T.vb[:]).then_inc(S.qv, 1)
+
+    t = g.tensor
+    for h in range(2):
+        pair = (2 * h, 2 * h + 1)
+        for i in pair:
+            t.wait_ge(S["qa%d" % i], 3 if i == 0 else 1)
+            t.matmul_mx(bank(i), blk(T.aq, i), blk(T.as_, i), T.xq[:], T.xs[:], True, True).then_inc(S["u%d" % i], 1)
+        for i in pair:
+            t.matmul_mx(bank(4 + i), blk(T.aq, i), blk(T.as_, i), T.eq[:], T.es[:], True, True).then_inc(S["d%d" % i], 1)
+    t.wait_ge(S.qt, 1)
+    t.wait_ge(S.qw, 1)
+    t.wait_ge(S.qv, 1)
+    for j in [me] + order:
+        if j != me:
+            t.wait_ge(S["arr%d" % j], 16)
+        t.matmul_mx(bank(4 + j), blk(T.tq, j), blk(T.ts, j), T.vq[:], T.vs[:], True, True).then_inc(S["z%d" % j], 1)
+        t.matmul_mx(bank(j), T.wq[:], T.ws[:], blk(T.tq, j), blk(T.ts, j), True, True).then_inc(S["y%d" % j], 1)
+
+    dests = [T.cores[(me + k) % N] for k in range(1, N)]
+    mask = topo.mask(core, dests[0])
+    ids = []
+    for d in dests:
+        mask &= topo.mask(core, d)
+        rid, pid = topo.addr(d, core)
+        ids.append(DstId(rid=rid, pnc=pid))
+    g.wait_ge(S.qt, 1)
+    for view in (blk(T.tq, me).bitcast(dt.uint8), blk(T.ts, me)):
+        g.remote_dma_fused([RemoteDMATransfer(dst_ids=ids, dma_engine_mask=mask, remote_sem=S["arr%d" % me],
+                                              srcs=[view], dsts=[view] * len(ids))], local_sem=S.sent)
+
+    for j in [me] + order:
+        k = 0 if j == me else 1 + run_of[j]
+        v.wait_ge(S["y%d" % j], 1)
+        v.tensor_copy(blk(T.oy, j), bank(j)).then_inc(S["cy%d" % k], 1)
+
+    def cols(r):
+        return slice(B * r[0], B * (r[-1] + 1))
+
+    nz = 0
+    for j in [me] + order:
+        k = 0 if j == me else 1 + run_of[j]
+        g.scalar.wait_ge(S["z%d" % j], 1)
+        g.scalar.activation(blk(T.oz, j), bank(4 + j), ActivationFunctionType.Copy).then_inc(S["cz%d" % k], 1)
+        if j != me:
+            r = runs[k - 1]
+            if j == max(r, key=order.index):
+                g.scalar.wait_ge(S["cz%d" % k], len(r))
+                g.scalar.dma_start(T.z[:, cols(r)], T.oz[:, cols(r)]).then_inc(S.stz, 16)
+                nz += 16
+
+    g.sync.wait_ge(S.cy0, 1)
+    g.sync.wait_ge(S.cz0, 1)
+    g.sync.wait_ge(S.sent, 16)
+    g.sync.dma_start(T.y[:, cols([me])], T.oy[:, cols([me])]).then_inc(S.sty, 16)
+    g.sync.dma_start(T.z[:, cols([me])], T.oz[:, cols([me])]).then_inc(S.sty, 16)
+    for k, r in enumerate(runs):
+        g.sync.wait_ge(S["cy%d" % (1 + k)], len(r))
+        g.sync.dma_start(T.y[:, cols(r)], T.oy[:, cols(r)]).then_inc(S.sty, 16)
+    g.sync.wait_ge(S.sty, 32 + 16 * len(runs))
+    g.scalar.wait_ge(S.stz, nz)

@@ -7,6 +7,7 @@ F = 4 * B
 BANK = 512
 C = 0.037
 CODES = "float8_e4m3fn_x4"
+PIECES = [(0, 1), (2, 3)]
 
 SCRATCH = {
     "xb": ("sbuf", [128, F], "bfloat16"),
@@ -15,6 +16,7 @@ SCRATCH = {
     "wb": ("sbuf", [128, F], "bfloat16"),
     "vb": ("sbuf", [128, F], "bfloat16"),
     "tb": ("sbuf", [128, F], "bfloat16"),
+    "sg": ("sbuf", [128, 2 * B], "float32"),
     "mk": ("sbuf", [128, 4 * B], "float32"),
     "oy": ("sbuf", [128, N * B], "float32"),
     "oz": ("sbuf", [128, N * B], "float32"),
@@ -27,11 +29,11 @@ SCRATCH = {
     "ps": ("psum", [128, 8 * BANK], "float32"),
 }
 SEMAPHORES = (
-    ["lx", "le", "la0", "la1", "lw", "lv"]
+    ["lx", "le", "lw", "lv"] + ["la%d" % i for i in range(len(PIECES))]
     + ["qa%d" % i for i in range(4)] + ["qt", "qw", "qv"]
     + ["u%d" % i for i in range(4)] + ["d%d" % i for i in range(4)]
-    + ["mk0", "mk1", "rt"]
-    + ["sent"] + ["arr%d" % j for j in range(N)]
+    + ["sg0", "sg1"] + ["mk%d" % i for i in range(4)] + ["rt"]
+    + ["sentp", "sentc"] + ["arr%d" % j for j in range(N)]
     + ["y%d" % j for j in range(N)] + ["z%d" % j for j in range(N)]
     + ["cy%d" % k for k in range(3)] + ["cz%d" % k for k in range(3)]
     + ["sty", "stz"]
@@ -50,36 +52,53 @@ def rank_program(g, core, T, topo):
     def bank(b):
         return T.ps[:, BANK * b:BANK * b + B]
 
-    order = [(me - k) % N for k in range(1, N)]
-    runs = [r for r in (list(range(0, me)), list(range(me + 1, N))) if r]
-    runs.sort(key=lambda r: max(order.index(j) for j in r))
+    order = [me ^ k for k in (2, 3, 1)]
+    runs = [sorted(order[:2]), order[2:]]
     run_of = {j: k for k, r in enumerate(runs) for j in r}
 
     g.sync.dma_start(T.xb[:], T.x[:]).then_inc(S.lx, 16)
     g.scalar.dma_start(T.eb[:], T.e[:]).then_inc(S.le, 16)
-    for h in range(2):
-        g.sync.dma_start(T.ab[:, 2 * F * h:2 * F * (h + 1)], T.a[:, 2 * F * h:2 * F * (h + 1)]).then_inc(S["la%d" % h], 16)
+    for h, p in enumerate(PIECES):
+        c = slice(F * p[0], F * (p[-1] + 1))
+        g.sync.dma_start(T.ab[:, c], T.a[:, c]).then_inc(S["la%d" % h], 16)
     g.scalar.wait_ge(S.lx, 16)
     g.scalar.dma_start(T.wb[:], T.w[:]).then_inc(S.lw, 16)
     g.scalar.dma_start(T.vb[:], T.v[:]).then_inc(S.lv, 16)
 
+    for i in PIECES[0]:
+        g.scalar.wait_ge(S["u%d" % i], 1)
+        g.scalar.activation(blk(T.sg, i), bank(i), ActivationFunctionType.Sign).then_inc(S["sg%d" % i], 1)
+    for i in PIECES[0]:
+        g.scalar.wait_ge(S["sg%d" % i], 1)
+        g.scalar.activation(blk(T.mk, i), blk(T.sg, i), ActivationFunctionType.Relu, scale=C).then_inc(S["mk%d" % i], 1)
+
     v = g.vector
+
+    def quantise(p):
+        for i in p:
+            v.quantize_mx(blk(T.aq, i), blk(T.as_, i), blk(T.ab, i, F)).then_inc(S["qa%d" % i], 1)
+
+    def masks(p):
+        for i in p:
+            v.wait_ge(S["u%d" % i], 1)
+            v.tensor_scalar(blk(T.mk, i), bank(i), 0.0, C, AluOpType.is_gt, AluOpType.mult).then_inc(S["mk%d" % i], 1)
+
+    def parts(p):
+        for i in p:
+            v.wait_ge(S["mk%d" % i], 1)
+            v.wait_ge(S["d%d" % i], 1)
+            v.tensor_tensor(T.tb[:, i:F:4], bank(4 + i), blk(T.mk, i), AluOpType.mult).then_inc(S.rt, 1)
+
     v.wait_ge(S.lx, 16)
     v.quantize_mx(T.xq[:], T.xs[:], T.xb[:]).then_inc(S.qa0, 1)
     v.wait_ge(S.le, 16)
     v.quantize_mx(T.eq[:], T.es[:], T.eb[:]).then_inc(S.qa0, 1)
-    for h in range(2):
-        pair = (2 * h, 2 * h + 1)
+    for h, p in enumerate(PIECES):
         v.wait_ge(S["la%d" % h], 16)
-        for i in pair:
-            v.quantize_mx(blk(T.aq, i), blk(T.as_, i), blk(T.ab, i, F)).then_inc(S["qa%d" % i], 1)
-        for i in pair:
-            v.wait_ge(S["u%d" % i], 1)
-            v.tensor_scalar(blk(T.mk, i), bank(i), 0.0, C, AluOpType.is_gt, AluOpType.mult).then_inc(S["mk%d" % h], 1)
-        v.wait_ge(S["mk%d" % h], 2)
-        for i in pair:
-            v.wait_ge(S["d%d" % i], 1)
-            v.tensor_tensor(T.tb[:, i:F:4], bank(4 + i), blk(T.mk, i), AluOpType.mult).then_inc(S.rt, 1)
+        quantise(p)
+    parts(PIECES[0])
+    masks(PIECES[1])
+    parts(PIECES[1])
     v.wait_ge(S.rt, 4)
     v.quantize_mx(blk(T.tq, me), blk(T.ts, me), T.tb[:]).then_inc(S.qt, 1)
     v.wait_ge(S.lw, 16)
@@ -88,12 +107,11 @@ def rank_program(g, core, T, topo):
     v.quantize_mx(T.vq[:], T.vs[:], T.vb[:]).then_inc(S.qv, 1)
 
     t = g.tensor
-    for h in range(2):
-        pair = (2 * h, 2 * h + 1)
-        for i in pair:
+    for p in PIECES:
+        for i in p:
             t.wait_ge(S["qa%d" % i], 3 if i == 0 else 1)
             t.matmul_mx(bank(i), blk(T.aq, i), blk(T.as_, i), T.xq[:], T.xs[:], True, True).then_inc(S["u%d" % i], 1)
-        for i in pair:
+        for i in p:
             t.matmul_mx(bank(4 + i), blk(T.aq, i), blk(T.as_, i), T.eq[:], T.es[:], True, True).then_inc(S["d%d" % i], 1)
     t.wait_ge(S.qt, 1)
     t.wait_ge(S.qw, 1)
@@ -104,7 +122,7 @@ def rank_program(g, core, T, topo):
         t.matmul_mx(bank(4 + j), blk(T.tq, j), blk(T.ts, j), T.vq[:], T.vs[:], True, True).then_inc(S["z%d" % j], 1)
         t.matmul_mx(bank(j), T.wq[:], T.ws[:], blk(T.tq, j), blk(T.ts, j), True, True).then_inc(S["y%d" % j], 1)
 
-    dests = [T.cores[(me + k) % N] for k in range(1, N)]
+    dests = [T.cores[j] for j in order]
     mask = topo.mask(core, dests[0])
     ids = []
     for d in dests:
@@ -112,37 +130,32 @@ def rank_program(g, core, T, topo):
         rid, pid = topo.addr(d, core)
         ids.append(DstId(rid=rid, pnc=pid))
     g.wait_ge(S.qt, 1)
-    for view in (blk(T.tq, me).bitcast(dt.uint8), blk(T.ts, me)):
+    for view, left in ((blk(T.ts, me), S.sentp), (blk(T.tq, me).bitcast(dt.uint8), S.sentc)):
         g.remote_dma_fused([RemoteDMATransfer(dst_ids=ids, dma_engine_mask=mask, remote_sem=S["arr%d" % me],
-                                              srcs=[view], dsts=[view] * len(ids))], local_sem=S.sent)
+                                              srcs=[view], dsts=[view] * len(ids))], local_sem=left)
+
+    def cols(r):
+        return slice(B * r[0], B * (r[-1] + 1))
 
     for j in [me] + order:
         k = 0 if j == me else 1 + run_of[j]
         v.wait_ge(S["y%d" % j], 1)
         v.tensor_copy(blk(T.oy, j), bank(j)).then_inc(S["cy%d" % k], 1)
-
-    def cols(r):
-        return slice(B * r[0], B * (r[-1] + 1))
-
-    nz = 0
-    for j in [me] + order:
-        k = 0 if j == me else 1 + run_of[j]
         g.scalar.wait_ge(S["z%d" % j], 1)
         g.scalar.activation(blk(T.oz, j), bank(4 + j), ActivationFunctionType.Copy).then_inc(S["cz%d" % k], 1)
-        if j != me:
+        if j in (order[1], order[2]):
             r = runs[k - 1]
-            if j == max(r, key=order.index):
-                g.scalar.wait_ge(S["cz%d" % k], len(r))
-                g.scalar.dma_start(T.z[:, cols(r)], T.oz[:, cols(r)]).then_inc(S.stz, 16)
-                nz += 16
+            g.scalar.wait_ge(S["cz%d" % k], len(r))
+            g.scalar.dma_start(T.z[:, cols(r)], T.oz[:, cols(r)]).then_inc(S.stz, 16)
 
     g.sync.wait_ge(S.cy0, 1)
     g.sync.wait_ge(S.cz0, 1)
-    g.sync.wait_ge(S.sent, 16)
     g.sync.dma_start(T.y[:, cols([me])], T.oy[:, cols([me])]).then_inc(S.sty, 16)
     g.sync.dma_start(T.z[:, cols([me])], T.oz[:, cols([me])]).then_inc(S.sty, 16)
     for k, r in enumerate(runs):
         g.sync.wait_ge(S["cy%d" % (1 + k)], len(r))
         g.sync.dma_start(T.y[:, cols(r)], T.oy[:, cols(r)]).then_inc(S.sty, 16)
+    g.sync.wait_ge(S.sentp, 8)
+    g.sync.wait_ge(S.sentc, 8)
     g.sync.wait_ge(S.sty, 32 + 16 * len(runs))
-    g.scalar.wait_ge(S.stz, nz)
+    g.scalar.wait_ge(S.stz, 16 * len(runs))

from concourse.bass import DstId, RemoteDMATransfer
from concourse.mybir import dt, AluOpType, ActivationFunctionType

N = 4
B = 128
F = 4 * B
BANK = 512
C = 0.037
CODES = "float8_e4m3fn_x4"
PIECES = [(0, 1), (2, 3)]

SCRATCH = {
    "xb": ("sbuf", [128, F], "bfloat16"),
    "eb": ("sbuf", [128, F], "bfloat16"),
    "ab": ("sbuf", [128, 4 * F], "bfloat16"),
    "wb": ("sbuf", [128, F], "bfloat16"),
    "vb": ("sbuf", [128, F], "bfloat16"),
    "tb": ("sbuf", [128, F], "bfloat16"),
    "sg": ("sbuf", [128, 2 * B], "float32"),
    "mk": ("sbuf", [128, 4 * B], "float32"),
    "oy": ("sbuf", [128, N * B], "float32"),
    "oz": ("sbuf", [128, N * B], "float32"),
    "xq": ("sbuf", [128, B], CODES), "xs": ("sbuf", [128, B], "uint8"),
    "eq": ("sbuf", [128, B], CODES), "es": ("sbuf", [128, B], "uint8"),
    "aq": ("sbuf", [128, 4 * B], CODES), "as_": ("sbuf", [128, 4 * B], "uint8"),
    "wq": ("sbuf", [128, B], CODES), "ws": ("sbuf", [128, B], "uint8"),
    "vq": ("sbuf", [128, B], CODES), "vs": ("sbuf", [128, B], "uint8"),
    "tq": ("sbuf", [128, N * B], CODES), "ts": ("sbuf", [128, N * B], "uint8"),
    "ps": ("psum", [128, 8 * BANK], "float32"),
}
SEMAPHORES = (
    ["lx", "le", "lw", "lv"] + ["la%d" % i for i in range(len(PIECES))]
    + ["qa%d" % i for i in range(4)] + ["qt", "qw", "qv"]
    + ["u%d" % i for i in range(4)] + ["d%d" % i for i in range(4)]
    + ["sg0", "sg1"] + ["mk%d" % i for i in range(4)] + ["rt"]
    + ["sentp", "sentc"] + ["arr%d" % j for j in range(N)]
    + ["y%d" % j for j in range(N)] + ["z%d" % j for j in range(N)]
    + ["cy%d" % k for k in range(3)] + ["cz%d" % k for k in range(3)]
    + ["sty", "stz"]
)


def rank_program(g, core, T, topo):
    me = T.rank_of(core)
    if me is None:
        return
    S = T.sem

    def blk(t, j, w=B):
        return t[:, w * j:w * j + w]

    def bank(b):
        return T.ps[:, BANK * b:BANK * b + B]

    order = [me ^ k for k in (2, 3, 1)]
    runs = [sorted(order[:2]), order[2:]]
    run_of = {j: k for k, r in enumerate(runs) for j in r}

    g.sync.dma_start(T.xb[:], T.x[:]).then_inc(S.lx, 16)
    g.scalar.dma_start(T.eb[:], T.e[:]).then_inc(S.le, 16)
    for h, p in enumerate(PIECES):
        c = slice(F * p[0], F * (p[-1] + 1))
        g.sync.dma_start(T.ab[:, c], T.a[:, c]).then_inc(S["la%d" % h], 16)
    g.scalar.wait_ge(S.lx, 16)
    g.scalar.dma_start(T.wb[:], T.w[:]).then_inc(S.lw, 16)
    g.scalar.dma_start(T.vb[:], T.v[:]).then_inc(S.lv, 16)

    for i in PIECES[0]:
        g.scalar.wait_ge(S["u%d" % i], 1)
        g.scalar.activation(blk(T.sg, i), bank(i), ActivationFunctionType.Sign).then_inc(S["sg%d" % i], 1)
    for i in PIECES[0]:
        g.scalar.wait_ge(S["sg%d" % i], 1)
        g.scalar.activation(blk(T.mk, i), blk(T.sg, i), ActivationFunctionType.Relu, scale=C).then_inc(S["mk%d" % i], 1)

    v = g.vector

    def quantise(p):
        for i in p:
            v.quantize_mx(blk(T.aq, i), blk(T.as_, i), blk(T.ab, i, F)).then_inc(S["qa%d" % i], 1)

    def masks(p):
        for i in p:
            v.wait_ge(S["u%d" % i], 1)
            v.tensor_scalar(blk(T.mk, i), bank(i), 0.0, C, AluOpType.is_gt, AluOpType.mult).then_inc(S["mk%d" % i], 1)

    def parts(p):
        for i in p:
            v.wait_ge(S["mk%d" % i], 1)
            v.wait_ge(S["d%d" % i], 1)
            v.tensor_tensor(T.tb[:, i:F:4], bank(4 + i), blk(T.mk, i), AluOpType.mult).then_inc(S.rt, 1)

    v.wait_ge(S.lx, 16)
    v.quantize_mx(T.xq[:], T.xs[:], T.xb[:]).then_inc(S.qa0, 1)
    v.wait_ge(S.le, 16)
    v.quantize_mx(T.eq[:], T.es[:], T.eb[:]).then_inc(S.qa0, 1)
    for h, p in enumerate(PIECES):
        v.wait_ge(S["la%d" % h], 16)
        quantise(p)
    parts(PIECES[0])
    masks(PIECES[1])
    parts(PIECES[1])
    v.wait_ge(S.rt, 4)
    v.quantize_mx(blk(T.tq, me), blk(T.ts, me), T.tb[:]).then_inc(S.qt, 1)
    v.wait_ge(S.lw, 16)
    v.quantize_mx(T.wq[:], T.ws[:], T.wb[:]).then_inc(S.qw, 1)
    v.wait_ge(S.lv, 16)
    v.quantize_mx(T.vq[:], T.vs[:], T.vb[:]).then_inc(S.qv, 1)

    t = g.tensor
    for p in PIECES:
        for i in p:
            t.wait_ge(S["qa%d" % i], 3 if i == 0 else 1)
            t.matmul_mx(bank(i), blk(T.aq, i), blk(T.as_, i), T.xq[:], T.xs[:], True, True).then_inc(S["u%d" % i], 1)
        for i in p:
            t.matmul_mx(bank(4 + i), blk(T.aq, i), blk(T.as_, i), T.eq[:], T.es[:], True, True).then_inc(S["d%d" % i], 1)
    t.wait_ge(S.qt, 1)
    t.wait_ge(S.qw, 1)
    t.wait_ge(S.qv, 1)
    for j in [me] + order:
        if j != me:
            t.wait_ge(S["arr%d" % j], 16)
        t.matmul_mx(bank(4 + j), blk(T.tq, j), blk(T.ts, j), T.vq[:], T.vs[:], True, True).then_inc(S["z%d" % j], 1)
        t.matmul_mx(bank(j), T.wq[:], T.ws[:], blk(T.tq, j), blk(T.ts, j), True, True).then_inc(S["y%d" % j], 1)

    dests = [T.cores[j] for j in order]
    mask = topo.mask(core, dests[0])
    ids = []
    for d in dests:
        mask &= topo.mask(core, d)
        rid, pid = topo.addr(d, core)
        ids.append(DstId(rid=rid, pnc=pid))
    g.wait_ge(S.qt, 1)
    for view, left in ((blk(T.ts, me), S.sentp), (blk(T.tq, me).bitcast(dt.uint8), S.sentc)):
        g.remote_dma_fused([RemoteDMATransfer(dst_ids=ids, dma_engine_mask=mask, remote_sem=S["arr%d" % me],
                                              srcs=[view], dsts=[view] * len(ids))], local_sem=left)

    def cols(r):
        return slice(B * r[0], B * (r[-1] + 1))

    for j in [me] + order:
        k = 0 if j == me else 1 + run_of[j]
        v.wait_ge(S["y%d" % j], 1)
        v.tensor_copy(blk(T.oy, j), bank(j)).then_inc(S["cy%d" % k], 1)
        g.scalar.wait_ge(S["z%d" % j], 1)
        g.scalar.activation(blk(T.oz, j), bank(4 + j), ActivationFunctionType.Copy).then_inc(S["cz%d" % k], 1)
        if j in (order[1], order[2]):
            r = runs[k - 1]
            g.scalar.wait_ge(S["cz%d" % k], len(r))
            g.scalar.dma_start(T.z[:, cols(r)], T.oz[:, cols(r)]).then_inc(S.stz, 16)

    g.sync.wait_ge(S.cy0, 1)
    g.sync.wait_ge(S.cz0, 1)
    g.sync.dma_start(T.y[:, cols([me])], T.oy[:, cols([me])]).then_inc(S.sty, 16)
    g.sync.dma_start(T.z[:, cols([me])], T.oz[:, cols([me])]).then_inc(S.sty, 16)
    for k, r in enumerate(runs):
        g.sync.wait_ge(S["cy%d" % (1 + k)], len(r))
        g.sync.dma_start(T.y[:, cols(r)], T.oy[:, cols(r)]).then_inc(S.sty, 16)
    g.sync.wait_ge(S.sentp, 8)
    g.sync.wait_ge(S.sentc, 8)
    g.sync.wait_ge(S.sty, 32 + 16 * len(runs))
    g.scalar.wait_ge(S.stz, 16 * len(runs))
